import numpy as np
import ml_dtypes


def mxq(x, axis, fmt="e4m3"):
    dtype, down = {"e4m3": (ml_dtypes.float8_e4m3fn, 7), "e5m2": (ml_dtypes.float8_e5m2, 14)}[fmt]
    v = np.moveaxis(np.asarray(x, np.float32).astype(ml_dtypes.bfloat16).astype(np.float64), axis, -1)
    blocks = v.reshape(v.shape[:-1] + (-1, 32))
    amax = np.abs(blocks).max(-1, keepdims=True)
    byte = np.maximum(np.where(amax > 0, np.frexp(amax)[1] - 1 + 127, 0) - down, 1)
    scale = np.exp2(byte - 127.0)
    codes = (blocks / scale).astype(np.float32).astype(dtype).astype(np.float64)
    return np.moveaxis((codes * scale).reshape(v.shape), -1, axis)


WIDE = False


def mx_kscale(k):
    if not WIDE:
        return np.ones(k)
    levels = np.array([10, -10, 5, -5, 0])
    if k % 512:
        return np.exp2(np.random.permutation(np.resize(levels, k // 32))).repeat(32)
    a = np.empty((k // 512, 16))
    for p in range(k // 512):
        a[p, :8] = np.random.permutation(np.resize(levels, 8))
        for g in range(8):
            far = levels[np.abs(levels - a[p, g]) >= 10]
            a[p, g + 8] = far[np.random.randint(len(far))]
    return np.exp2(a.ravel()).repeat(32)


def f64(x):
    return np.asarray(x).astype(np.float64)


def striped(idx):
    return np.tile(np.asarray(idx).reshape(-1, 16).T, (8, 1)).astype(np.uint16)


def unstriped(offs):
    return offs[:16].T.reshape(-1).astype(np.int64)


E2M1 = np.array([0.0, 0.5, 1.0, 1.5, 2.0, 3.0, 4.0, 6.0, -0.0, -0.5, -1.0, -1.5, -2.0, -3.0, -4.0, -6.0])


def pack_weight(w, fmt):
    k, n = w.shape
    w = f64(np.asarray(w, np.float32).astype(ml_dtypes.bfloat16)).reshape(k // 32, 32, n)
    amax = np.abs(w).max(1)
    if fmt == "e4m3":
        byte = np.frexp(amax)[1] - 1 + 127 - 7
    else:
        mant, ex = np.frexp(amax / 6.0)
        byte = np.where(mant > 0.5, ex, ex - 1) + 127
    byte = np.clip(np.where(amax > 0, byte, 1), 1, 254)
    scaled = (w * np.exp2(127.0 - byte)[:, None, :]).reshape(k, n).astype(np.float32)
    by_word = np.ascontiguousarray(scaled.reshape(k // 512, 128, 4, n).transpose(0, 1, 3, 2))
    if fmt == "e4m3":
        words = by_word.astype(ml_dtypes.float8_e4m3fn).view(np.uint8)
    else:
        c = by_word.astype(ml_dtypes.float4_e2m1fn).view(np.uint8) & 0xF
        words = (c[..., 0::2] | (c[..., 1::2] << 4)).reshape(k // 512, 128, 2 * n)
    return np.ascontiguousarray(words), np.ascontiguousarray(byte.astype(np.uint8).reshape(k // 512, 16, n))


def unpack_weight(words, scales, fmt):
    g, _, n = scales.shape
    words = np.ascontiguousarray(words).reshape(g, 128, n, -1)
    if fmt == "e4m3":
        vals = words.view(ml_dtypes.float8_e4m3fn).astype(np.float64)
    else:
        nib = np.empty((g, 128, n, 4), np.uint8)
        nib[..., 0::2] = words & 0xF
        nib[..., 1::2] = words >> 4
        vals = E2M1[nib]
    vals = vals * np.repeat(np.exp2(scales.astype(np.float64) - 127.0), 8, axis=1)[..., None]
    return vals.transpose(0, 1, 3, 2).reshape(g * 512, n)


def sigmoid(v):
    return 1.0 / (1.0 + np.exp(-v))


K, R, F, T, J, G = 512, 128, 512, 2048, 512, 128


def setup_inputs():
    n = np.random.standard_normal
    idx = np.random.permutation(T)[:J]
    fk = mx_kscale(K)
    tabp = pack_weight(n((K, T)) / fk[:, None], "e4m3")
    dtabp = pack_weight(n((K, T)) / fk[:, None], "e4m3")
    return {
        "tab_words": tabp[0],
        "tab_scales": tabp[1],
        "dtab_words": dtabp[0],
        "dtab_scales": dtabp[1],
        "w1": (n((K, R)) * 1 / np.sqrt(K) * fk[:, None]).astype(np.float32),
        "temper": (np.random.uniform(0.5, 2.0, (R, 1))).astype(np.float32),
        "og": (np.random.uniform(0.5, 2.0, (R, 1))).astype(np.float32),
        "base": (0.3 * n((R, G))).astype(np.float32),
        "offs": striped(idx),
    }


def reference(tab_words, tab_scales, dtab_words, dtab_scales, w1, temper, og, base, offs):
    idx = unstriped(offs)
    tabu = unpack_weight(tab_words, tab_scales, "e4m3")
    dtabu = unpack_weight(dtab_words, dtab_scales, "e4m3")
    w1q = mxq(f64(w1), 0, "e4m3")
    tabidxg = tabu[:, idx]
    a = w1q.T @ tabidxg
    dtabidxg = dtabu[:, idx]
    ta = w1q.T @ dtabidxg
    p = np.exp(a * f64(temper))
    z = p.reshape(R, G, J // G).sum(axis=2)
    s = np.log(z) / f64(temper)
    tp = ta * f64(temper) * p
    tz = tp.reshape(R, G, J // G).sum(axis=2)
    ts = tz / z / f64(temper)
    tu1 = ts * sigmoid(s) * (1.0 + s * (1.0 - sigmoid(s)))
    y = tu1 * f64(og) + f64(base)
    return y

@@ -1,0 +1,146 @@
+from contextlib import ExitStack
+
+import concourse.mybir as mybir
+from concourse.masks import make_identity
+
+K, R, T, J, G = 512, 128, 2048, 512, 128
+FLOPS = 2 * 2 * K * R * J
+
+F32 = mybir.dt.float32
+BF16 = mybir.dt.bfloat16
+I32 = mybir.dt.int32
+U32 = mybir.dt.uint32
+U16 = mybir.dt.uint16
+U8 = mybir.dt.uint8
+FP8X4 = mybir.dt.float8_e4m3fn_x4
+ALU = mybir.AluOpType
+ACT = mybir.ActivationFunctionType
+AX = mybir.AxisListType
+
+P = 128
+PACK = 4
+POOL = J // G
+HALVES = 2
+JH = J // HALVES
+GH = G // HALVES
+LIST_COLS = JH // 16
+DTAB_ROW0 = 4
+
+
+def load_scale_rows(queue, plane, scales, row0):
+    for r in range(4):
+        queue.dma_start(out=plane[row0 + r : P : 32, :].bitcast(I32), in_=scales[0, r:16:4, :].bitcast(I32))
+
+
+def tile_attend_tcsoftmaxpool_kernel(tc, tab_words, tab_scales, dtab_words, dtab_scales, w1, temper, og, base, offs, out):
+    nc = tc.nc
+    with ExitStack() as ctx:
+        sb = ctx.enter_context(tc.tile_pool(name="sb", bufs=1))
+        ps = ctx.enter_context(tc.psum_pool(name="ps", bufs=1))
+
+        offsets = sb.tile([P, J // 16], U16, name="offsets")
+        tab_plane = sb.tile([P, T], U8, name="tab_plane", align_bytes=64)
+        dtab_plane = sb.tile([P, T], U8, name="dtab_plane", tag="dtab_plane", align_bytes=64)
+        tab_sb = sb.tile([P, T], I32, name="tab_sb", align_bytes=64)
+        w_raw = sb.tile([P, PACK, R], F32, name="w_raw", tag="dtab_sb", align_bytes=64)
+        temper_sb = sb.tile([P, 1], F32, name="temper_sb")
+
+        nc.vector.memset(tab_plane[:].bitcast(I32), 0)
+        nc.vector.memset(dtab_plane[:].bitcast(I32), 0)
+
+        nc.sync.dma_start(offsets[:], offs)
+        nc.scalar.dma_start(out=w_raw[:], in_=w1.rearrange("(p j) r -> p j r", j=PACK))
+        nc.sync.dma_start(out=temper_sb[:], in_=temper)
+        nc.scalar.dma_start(out=tab_sb[:], in_=tab_words[0].rearrange("p n t -> p (n t)").bitcast(I32))
+        load_scale_rows(nc.sync, tab_plane, tab_scales, 0)
+        load_scale_rows(nc.sync, dtab_plane, dtab_scales, DTAB_ROW0)
+
+        w_bf = sb.tile([P, R, PACK], BF16, name="w_bf", tag="w_bf", align_bytes=64)
+        w_codes = sb.tile([P, R], U32, name="w_codes", align_bytes=64)
+        w_scales = sb.tile([P, R], U8, name="w_scales", align_bytes=64)
+        nc.scalar.copy(out=w_bf[:], in_=w_raw[:].rearrange("p j r -> p r j"))
+        dtab_sb = sb.tile([P, T], I32, name="dtab_sb", tag="dtab_sb", align_bytes=64)
+        nc.scalar.dma_start(out=dtab_sb[:], in_=dtab_words[0].rearrange("p n t -> p (n t)").bitcast(I32))
+
+        tab_gs = sb.tile([P, J], U8, name="tab_gs", tag="tab_gs", align_bytes=64)
+        nc.vector.tensor_copy(tab_gs[:], tab_plane[:].indirect(offsets[:]))
+        nc.vector.quantize_mx(out=w_codes[:].bitcast(FP8X4), scales=w_scales[:], in_=w_bf[:].rearrange("p r j -> p (r j)"))
+        inv_temper = sb.tile([P, 1], F32, name="inv_temper")
+        nc.vector.reciprocal(inv_temper[:], temper_sb[:])
+
+        def product(name, words, gathered_scales, row0, h):
+            picked = sb.tile([P, JH], U32, name=name + "_picked%d" % h, tag=name + "_picked%d" % h, align_bytes=64)
+            nc.vector.tensor_copy(picked[:], words[:].bitcast(U32).indirect(offsets[:, h * LIST_COLS : (h + 1) * LIST_COLS]))
+            acc = ps.tile([P, 2 * JH], F32, name=name + "_acc%d" % h)
+            nc.tensor.matmul_mx(
+                out=acc[:, 0:JH],
+                lhsT=w_codes[:].bitcast(FP8X4),
+                lhsT_scale=w_scales[:],
+                rhs=picked[:].bitcast(FP8X4),
+                rhs_scale=gathered_scales[row0:P, h * JH : (h + 1) * JH],
+                start=True,
+                stop=True,
+            )
+            return acc
+
+        ident = sb.tile([P, P], F32, name="ident")
+        make_identity(nc, ident[:])
+
+        a = [product("a", tab_sb, tab_gs, 0, h) for h in range(HALVES)]
+        base_sb = sb.tile([P, G], F32, name="base_sb", tag="w_bf", align_bytes=64)
+        nc.sync.dma_start(out=base_sb[:], in_=base)
+        og_sb = sb.tile([P, 1], F32, name="og_sb", tag="tab_gs", align_bytes=64)
+        nc.sync.dma_start(out=og_sb[:], in_=og)
+        top = sb.tile([P, G], F32, name="top")
+        p = sb.tile([P, POOL, G], F32, name="p")
+        halves = [slice(h * GH, (h + 1) * GH) for h in range(HALVES)]
+        for h in range(HALVES):
+            nc.vector.tensor_reduce(out=top[:, halves[h]], in_=a[h][:, 0:JH].rearrange("r (g t) -> r g t", t=POOL), axis=AX.X, op=ALU.max)
+        for h in range(HALVES):
+            below = sb.tile([P, POOL, GH], F32, name="below%d" % h, tag="below%d" % h, align_bytes=64)
+            nc.vector.tensor_tensor(
+                below[:],
+                a[h][:, 0:JH].rearrange("r (g t) -> r t g", t=POOL),
+                top[:, halves[h]].unsqueeze(1).to_broadcast([P, POOL, GH]),
+                ALU.subtract,
+            )
+            nc.scalar.activation(p[:, :, halves[h]], below[:], ACT.Exp, scale=temper_sb[:])
+
+        z_t = ps.tile([P, R], F32, name="z_t")
+        for t in range(POOL):
+            nc.tensor.matmul(z_t[:], lhsT=p[:, t, :], rhs=ident[:], is_transpose=True, start=(t == 0), stop=(t == POOL - 1))
+        log_z_t = sb.tile([P, R], F32, name="log_z_t")
+        nc.scalar.activation(log_z_t[:], z_t[:], ACT.Ln)
+
+        dtab_gs = sb.tile([P, J], U8, name="dtab_gs", tag="a_picked1", align_bytes=64)
+        nc.vector.tensor_copy(dtab_gs[:], dtab_plane[:].indirect(offsets[:]))
+        ta = [product("ta", dtab_sb, dtab_gs, DTAB_ROW0, h) for h in range(HALVES)]
+
+        tp = sb.tile([P, POOL, G], F32, name="tp")
+        for h in range(HALVES):
+            nc.vector.tensor_tensor(tp[:, :, halves[h]], ta[h][:, 0:JH].rearrange("r (g t) -> r t g", t=POOL), p[:, :, halves[h]], ALU.mult)
+        log_z = ta[0][:, JH : JH + G]
+        nc.tensor.transpose(log_z, log_z_t[:], ident[:])
+        s = sb.tile([P, G], F32, name="s")
+        nc.vector.scalar_tensor_tensor(s[:], log_z, inv_temper[:], top[:], ALU.mult, ALU.add)
+        pairs = sb.tile([P, 2, G], F32, name="pairs")
+        nc.vector.tensor_tensor(pairs[:], tp[:, 0:2, :], tp[:, 2:4, :], ALU.add)
+        tz = sb.tile([P, G], F32, name="tz")
+        nc.vector.tensor_tensor(tz[:], pairs[:, 0, :], pairs[:, 1, :], ALU.add)
+
+        inv_z = sb.tile([P, G], F32, name="inv_z")
+        th = sb.tile([P, G], F32, name="th")
+        nc.scalar.activation(inv_z[:], log_z, ACT.Exp, scale=-1.0)
+        nc.scalar.activation(th[:], s[:], ACT.Tanh, scale=0.5)
+
+        gained = sb.tile([P, G], F32, name="gained")
+        nc.vector.scalar_tensor_tensor(gained[:], inv_z[:], og_sb[:], tz[:], ALU.mult, ALU.mult)
+        slope = sb.tile([P, G], F32, name="slope")
+        nc.vector.scalar_tensor_tensor(slope[:], th[:], -1.0, s[:], ALU.add, ALU.mult)
+        gate = sb.tile([P, G], F32, name="gate")
+        nc.vector.scalar_tensor_tensor(gate[:], th[:], 1.0, gained[:], ALU.add, ALU.mult)
+        scaled = sb.tile([P, G], F32, name="scaled")
+        nc.vector.scalar_tensor_tensor(scaled[:], slope[:], -2.0, gate[:], ALU.add, ALU.mult)
+        result = sb.tile([P, G], F32, name="result")
+        nc.vector.scalar_tensor_tensor(result[:], scaled[:], -0.25, base_sb[:], ALU.mult, ALU.add)
+        nc.sync.dma_start(out=out, in_=result[:])

@@ -42,25 +42,29 @@ def tile_attend_tcsoftmaxpool_kernel(tc, tab_words, tab_scales, dtab_words, dtab
         tab_plane = sb.tile([P, T], U8, name="tab_plane", align_bytes=64)
         dtab_plane = sb.tile([P, T], U8, name="dtab_plane", tag="dtab_plane", align_bytes=64)
         tab_sb = sb.tile([P, T], I32, name="tab_sb", align_bytes=64)
-        w_raw = sb.tile([P, PACK, R], F32, name="w_raw", tag="dtab_sb", align_bytes=64)
+        dtab_sb = sb.tile([P, T], I32, name="dtab_sb", align_bytes=64)
+        w_raw = sb.tile([P, PACK, R], F32, name="w_raw")
+        og_sb = sb.tile([P, 1], F32, name="og_sb")
+        base_sb = sb.tile([P, G], F32, name="base_sb")
         temper_sb = sb.tile([P, 1], F32, name="temper_sb")
 
         nc.vector.memset(tab_plane[:].bitcast(I32), 0)
         nc.vector.memset(dtab_plane[:].bitcast(I32), 0)
 
         nc.sync.dma_start(offsets[:], offs)
-        nc.scalar.dma_start(out=w_raw[:], in_=w1.rearrange("(p j) r -> p j r", j=PACK))
-        nc.sync.dma_start(out=temper_sb[:], in_=temper)
-        nc.scalar.dma_start(out=tab_sb[:], in_=tab_words[0].rearrange("p n t -> p (n t)").bitcast(I32))
+        nc.sync.dma_start(out=w_raw[:], in_=w1.rearrange("(p j) r -> p j r", j=PACK))
         load_scale_rows(nc.sync, tab_plane, tab_scales, 0)
+        nc.sync.dma_start(out=tab_sb[:], in_=tab_words[0].rearrange("p n t -> p (n t)").bitcast(I32))
+        nc.sync.dma_start(out=temper_sb[:], in_=temper)
         load_scale_rows(nc.sync, dtab_plane, dtab_scales, DTAB_ROW0)
+        nc.sync.dma_start(out=dtab_sb[:], in_=dtab_words[0].rearrange("p n t -> p (n t)").bitcast(I32))
+        nc.sync.dma_start(out=og_sb[:], in_=og)
+        nc.sync.dma_start(out=base_sb[:], in_=base)
 
         w_bf = sb.tile([P, R, PACK], BF16, name="w_bf", tag="w_bf", align_bytes=64)
         w_codes = sb.tile([P, R], U32, name="w_codes", align_bytes=64)
         w_scales = sb.tile([P, R], U8, name="w_scales", align_bytes=64)
         nc.scalar.copy(out=w_bf[:], in_=w_raw[:].rearrange("p j r -> p r j"))
-        dtab_sb = sb.tile([P, T], I32, name="dtab_sb", tag="dtab_sb", align_bytes=64)
-        nc.scalar.dma_start(out=dtab_sb[:], in_=dtab_words[0].rearrange("p n t -> p (n t)").bitcast(I32))
 
         tab_gs = sb.tile([P, J], U8, name="tab_gs", tag="tab_gs", align_bytes=64)
         nc.vector.tensor_copy(tab_gs[:], tab_plane[:].indirect(offsets[:]))
@@ -87,10 +91,6 @@ def tile_attend_tcsoftmaxpool_kernel(tc, tab_words, tab_scales, dtab_words, dtab
         make_identity(nc, ident[:])
 
         a = [product("a", tab_sb, tab_gs, 0, h) for h in range(HALVES)]
-        base_sb = sb.tile([P, G], F32, name="base_sb", tag="w_bf", align_bytes=64)
-        nc.sync.dma_start(out=base_sb[:], in_=base)
-        og_sb = sb.tile([P, 1], F32, name="og_sb", tag="tab_gs", align_bytes=64)
-        nc.sync.dma_start(out=og_sb[:], in_=og)
         top = sb.tile([P, G], F32, name="top")
         p = sb.tile([P, POOL, G], F32, name="p")
         halves = [slice(h * GH, (h + 1) * GH) for h in range(HALVES)]
@@ -134,13 +134,17 @@ def tile_attend_tcsoftmaxpool_kernel(tc, tab_words, tab_scales, dtab_words, dtab
         nc.scalar.activation(th[:], s[:], ACT.Tanh, scale=0.5)
 
         gained = sb.tile([P, G], F32, name="gained")
-        nc.vector.scalar_tensor_tensor(gained[:], inv_z[:], og_sb[:], tz[:], ALU.mult, ALU.mult)
         slope = sb.tile([P, G], F32, name="slope")
-        nc.vector.scalar_tensor_tensor(slope[:], th[:], -1.0, s[:], ALU.add, ALU.mult)
         gate = sb.tile([P, G], F32, name="gate")
-        nc.vector.scalar_tensor_tensor(gate[:], th[:], 1.0, gained[:], ALU.add, ALU.mult)
         scaled = sb.tile([P, G], F32, name="scaled")
-        nc.vector.scalar_tensor_tensor(scaled[:], slope[:], -2.0, gate[:], ALU.add, ALU.mult)
         result = sb.tile([P, G], F32, name="result")
-        nc.vector.scalar_tensor_tensor(result[:], scaled[:], -0.25, base_sb[:], ALU.mult, ALU.add)
+        nc.vector.scalar_tensor_tensor(gained[:], inv_z[:], og_sb[:], tz[:], ALU.mult, ALU.mult)
+        for c in halves:
+            nc.vector.scalar_tensor_tensor(slope[:, c], th[:, c], -1.0, s[:, c], ALU.add, ALU.mult)
+        for c in halves:
+            nc.vector.scalar_tensor_tensor(gate[:, c], th[:, c], 1.0, gained[:, c], ALU.add, ALU.mult)
+        for c in halves:
+            nc.vector.scalar_tensor_tensor(scaled[:, c], slope[:, c], -2.0, gate[:, c], ALU.add, ALU.mult)
+        for c in halves:
+            nc.vector.scalar_tensor_tensor(result[:, c], scaled[:, c], -0.25, base_sb[:, c], ALU.mult, ALU.add)
         nc.sync.dma_start(out=out, in_=result[:])

@@ -88,7 +88,8 @@ def tile_attend_tcsoftmaxpool_kernel(tc, tab_words, tab_scales, dtab_words, dtab
             return acc
 
         ident = sb.tile([P, P], F32, name="ident")
-        make_identity(nc, ident[:])
+        nc.vector.memset(ident[:], 0.0)
+        make_identity(nc, ident[:], nomemset=True)
 
         a = [product("a", tab_sb, tab_gs, 0, h) for h in range(HALVES)]
         top = sb.tile([P, G], F32, name="top")
@@ -96,15 +97,17 @@ def tile_attend_tcsoftmaxpool_kernel(tc, tab_words, tab_scales, dtab_words, dtab
         halves = [slice(h * GH, (h + 1) * GH) for h in range(HALVES)]
         for h in range(HALVES):
             nc.vector.tensor_reduce(out=top[:, halves[h]], in_=a[h][:, 0:JH].rearrange("r (g t) -> r g t", t=POOL), axis=AX.X, op=ALU.max)
-        for h in range(HALVES):
-            below = sb.tile([P, POOL, GH], F32, name="below%d" % h, tag="below%d" % h, align_bytes=64)
+        pieces = [(0, GH), (GH, GH + GH // 2), (GH + GH // 2, G)]
+        for lo, hi in pieces:
+            h = lo // GH
+            below = sb.tile([P, POOL, hi - lo], F32, name="below%d" % lo)
             nc.vector.tensor_tensor(
                 below[:],
-                a[h][:, 0:JH].rearrange("r (g t) -> r t g", t=POOL),
-                top[:, halves[h]].unsqueeze(1).to_broadcast([P, POOL, GH]),
+                a[h][:, (lo - h * GH) * POOL : (hi - h * GH) * POOL].rearrange("r (g t) -> r t g", t=POOL),
+                top[:, lo:hi].unsqueeze(1).to_broadcast([P, POOL, hi - lo]),
                 ALU.subtract,
             )
-            nc.scalar.activation(p[:, :, halves[h]], below[:], ACT.Exp, scale=temper_sb[:])
+            nc.scalar.activation(p[:, :, lo:hi], below[:], ACT.Exp, scale=temper_sb[:])
 
         z_t = ps.tile([P, R], F32, name="z_t")
         for t in range(POOL):
@@ -121,12 +124,14 @@ def tile_attend_tcsoftmaxpool_kernel(tc, tab_words, tab_scales, dtab_words, dtab
             nc.vector.tensor_tensor(tp[:, :, halves[h]], ta[h][:, 0:JH].rearrange("r (g t) -> r t g", t=POOL), p[:, :, halves[h]], ALU.mult)
         log_z = ta[0][:, JH : JH + G]
         nc.tensor.transpose(log_z, log_z_t[:], ident[:])
+        pairs = sb.tile([P, 2, G], F32, name="pairs")
+        for c in halves:
+            nc.vector.tensor_tensor(pairs[:, :, c], tp[:, 0:2, c], tp[:, 2:4, c], ALU.add)
         s = sb.tile([P, G], F32, name="s")
         nc.vector.scalar_tensor_tensor(s[:], log_z, inv_temper[:], top[:], ALU.mult, ALU.add)
-        pairs = sb.tile([P, 2, G], F32, name="pairs")
-        nc.vector.tensor_tensor(pairs[:], tp[:, 0:2, :], tp[:, 2:4, :], ALU.add)
         tz = sb.tile([P, G], F32, name="tz")
-        nc.vector.tensor_tensor(tz[:], pairs[:, 0, :], pairs[:, 1, :], ALU.add)
+        for c in halves:
+            nc.vector.tensor_tensor(tz[:, c], pairs[:, 0, c], pairs[:, 1, c], ALU.add)
 
         inv_z = sb.tile([P, G], F32, name="inv_z")
         th = sb.tile([P, G], F32, name="th")

from contextlib import ExitStack

import concourse.mybir as mybir
from concourse.masks import make_identity

K, R, T, J, G = 512, 128, 2048, 512, 128
FLOPS = 2 * 2 * K * R * J

F32 = mybir.dt.float32
BF16 = mybir.dt.bfloat16
I32 = mybir.dt.int32
U32 = mybir.dt.uint32
U16 = mybir.dt.uint16
U8 = mybir.dt.uint8
FP8X4 = mybir.dt.float8_e4m3fn_x4
ALU = mybir.AluOpType
ACT = mybir.ActivationFunctionType
AX = mybir.AxisListType

P = 128
PACK = 4
POOL = J // G
HALVES = 2
JH = J // HALVES
GH = G // HALVES
LIST_COLS = JH // 16
DTAB_ROW0 = 4


def load_scale_rows(queue, plane, scales, row0):
    for r in range(4):
        queue.dma_start(out=plane[row0 + r : P : 32, :].bitcast(I32), in_=scales[0, r:16:4, :].bitcast(I32))


def tile_attend_tcsoftmaxpool_kernel(tc, tab_words, tab_scales, dtab_words, dtab_scales, w1, temper, og, base, offs, out):
    nc = tc.nc
    with ExitStack() as ctx:
        sb = ctx.enter_context(tc.tile_pool(name="sb", bufs=1))
        ps = ctx.enter_context(tc.psum_pool(name="ps", bufs=1))

        offsets = sb.tile([P, J // 16], U16, name="offsets")
        tab_plane = sb.tile([P, T], U8, name="tab_plane", align_bytes=64)
        dtab_plane = sb.tile([P, T], U8, name="dtab_plane", tag="dtab_plane", align_bytes=64)
        tab_sb = sb.tile([P, T], I32, name="tab_sb", align_bytes=64)
        dtab_sb = sb.tile([P, T], I32, name="dtab_sb", align_bytes=64)
        w_raw = sb.tile([P, PACK, R], F32, name="w_raw")
        og_sb = sb.tile([P, 1], F32, name="og_sb")
        base_sb = sb.tile([P, G], F32, name="base_sb")
        temper_sb = sb.tile([P, 1], F32, name="temper_sb")

        nc.vector.memset(tab_plane[:].bitcast(I32), 0)
        nc.vector.memset(dtab_plane[:].bitcast(I32), 0)

        nc.sync.dma_start(offsets[:], offs)
        nc.sync.dma_start(out=w_raw[:], in_=w1.rearrange("(p j) r -> p j r", j=PACK))
        load_scale_rows(nc.sync, tab_plane, tab_scales, 0)
        nc.sync.dma_start(out=tab_sb[:], in_=tab_words[0].rearrange("p n t -> p (n t)").bitcast(I32))
        nc.sync.dma_start(out=temper_sb[:], in_=temper)
        load_scale_rows(nc.sync, dtab_plane, dtab_scales, DTAB_ROW0)
        nc.sync.dma_start(out=dtab_sb[:], in_=dtab_words[0].rearrange("p n t -> p (n t)").bitcast(I32))
        nc.sync.dma_start(out=og_sb[:], in_=og)
        nc.sync.dma_start(out=base_sb[:], in_=base)

        w_bf = sb.tile([P, R, PACK], BF16, name="w_bf", tag="w_bf", align_bytes=64)
        w_codes = sb.tile([P, R], U32, name="w_codes", align_bytes=64)
        w_scales = sb.tile([P, R], U8, name="w_scales", align_bytes=64)
        nc.scalar.copy(out=w_bf[:], in_=w_raw[:].rearrange("p j r -> p r j"))

        tab_gs = sb.tile([P, J], U8, name="tab_gs", tag="tab_gs", align_bytes=64)
        nc.vector.tensor_copy(tab_gs[:], tab_plane[:].indirect(offsets[:]))
        nc.vector.quantize_mx(out=w_codes[:].bitcast(FP8X4), scales=w_scales[:], in_=w_bf[:].rearrange("p r j -> p (r j)"))
        inv_temper = sb.tile([P, 1], F32, name="inv_temper")
        nc.vector.reciprocal(inv_temper[:], temper_sb[:])

        def product(name, words, gathered_scales, row0, h):
            picked = sb.tile([P, JH], U32, name=name + "_picked%d" % h, tag=name + "_picked%d" % h, align_bytes=64)
            nc.vector.tensor_copy(picked[:], words[:].bitcast(U32).indirect(offsets[:, h * LIST_COLS : (h + 1) * LIST_COLS]))
            acc = ps.tile([P, 2 * JH], F32, name=name + "_acc%d" % h)
            nc.tensor.matmul_mx(
                out=acc[:, 0:JH],
                lhsT=w_codes[:].bitcast(FP8X4),
                lhsT_scale=w_scales[:],
                rhs=picked[:].bitcast(FP8X4),
                rhs_scale=gathered_scales[row0:P, h * JH : (h + 1) * JH],
                start=True,
                stop=True,
            )
            return acc

        ident = sb.tile([P, P], F32, name="ident")
        nc.vector.memset(ident[:], 0.0)
        make_identity(nc, ident[:], nomemset=True)

        a = [product("a", tab_sb, tab_gs, 0, h) for h in range(HALVES)]
        top = sb.tile([P, G], F32, name="top")
        p = sb.tile([P, POOL, G], F32, name="p")
        halves = [slice(h * GH, (h + 1) * GH) for h in range(HALVES)]
        for h in range(HALVES):
            nc.vector.tensor_reduce(out=top[:, halves[h]], in_=a[h][:, 0:JH].rearrange("r (g t) -> r g t", t=POOL), axis=AX.X, op=ALU.max)
        pieces = [(0, GH), (GH, GH + GH // 2), (GH + GH // 2, G)]
        for lo, hi in pieces:
            h = lo // GH
            below = sb.tile([P, POOL, hi - lo], F32, name="below%d" % lo)
            nc.vector.tensor_tensor(
                below[:],
                a[h][:, (lo - h * GH) * POOL : (hi - h * GH) * POOL].rearrange("r (g t) -> r t g", t=POOL),
                top[:, lo:hi].unsqueeze(1).to_broadcast([P, POOL, hi - lo]),
                ALU.subtract,
            )
            nc.scalar.activation(p[:, :, lo:hi], below[:], ACT.Exp, scale=temper_sb[:])

        z_t = ps.tile([P, R], F32, name="z_t")
        for t in range(POOL):
            nc.tensor.matmul(z_t[:], lhsT=p[:, t, :], rhs=ident[:], is_transpose=True, start=(t == 0), stop=(t == POOL - 1))
        log_z_t = sb.tile([P, R], F32, name="log_z_t")
        nc.scalar.activation(log_z_t[:], z_t[:], ACT.Ln)

        dtab_gs = sb.tile([P, J], U8, name="dtab_gs", tag="a_picked1", align_bytes=64)
        nc.vector.tensor_copy(dtab_gs[:], dtab_plane[:].indirect(offsets[:]))
        ta = [product("ta", dtab_sb, dtab_gs, DTAB_ROW0, h) for h in range(HALVES)]

        tp = sb.tile([P, POOL, G], F32, name="tp")
        for h in range(HALVES):
            nc.vector.tensor_tensor(tp[:, :, halves[h]], ta[h][:, 0:JH].rearrange("r (g t) -> r t g", t=POOL), p[:, :, halves[h]], ALU.mult)
        log_z = ta[0][:, JH : JH + G]
        nc.tensor.transpose(log_z, log_z_t[:], ident[:])
        pairs = sb.tile([P, 2, G], F32, name="pairs")
        for c in halves:
            nc.vector.tensor_tensor(pairs[:, :, c], tp[:, 0:2, c], tp[:, 2:4, c], ALU.add)
        s = sb.tile([P, G], F32, name="s")
        nc.vector.scalar_tensor_tensor(s[:], log_z, inv_temper[:], top[:], ALU.mult, ALU.add)
        tz = sb.tile([P, G], F32, name="tz")
        for c in halves:
            nc.vector.tensor_tensor(tz[:, c], pairs[:, 0, c], pairs[:, 1, c], ALU.add)

        inv_z = sb.tile([P, G], F32, name="inv_z")
        th = sb.tile([P, G], F32, name="th")
        nc.scalar.activation(inv_z[:], log_z, ACT.Exp, scale=-1.0)
        nc.scalar.activation(th[:], s[:], ACT.Tanh, scale=0.5)

        gained = sb.tile([P, G], F32, name="gained")
        slope = sb.tile([P, G], F32, name="slope")
        gate = sb.tile([P, G], F32, name="gate")
        scaled = sb.tile([P, G], F32, name="scaled")
        result = sb.tile([P, G], F32, name="result")
        nc.vector.scalar_tensor_tensor(gained[:], inv_z[:], og_sb[:], tz[:], ALU.mult, ALU.mult)
        for c in halves:
            nc.vector.scalar_tensor_tensor(slope[:, c], th[:, c], -1.0, s[:, c], ALU.add, ALU.mult)
        for c in halves:
            nc.vector.scalar_tensor_tensor(gate[:, c], th[:, c], 1.0, gained[:, c], ALU.add, ALU.mult)
        for c in halves:
            nc.vector.scalar_tensor_tensor(scaled[:, c], slope[:, c], -2.0, gate[:, c], ALU.add, ALU.mult)
        for c in halves:
            nc.vector.scalar_tensor_tensor(result[:, c], scaled[:, c], -0.25, base_sb[:, c], ALU.mult, ALU.add)
        nc.sync.dma_start(out=out, in_=result[:])
